import numpy as np
CORES = [31,71,111]
N = 3
T, CAP = 4096, 256
def entries(a): return a.T.reshape(-1)
def pack(v, P): return np.ascontiguousarray(np.asarray(v, np.int32).reshape(-1, P).T)
def lists(rng, how):
    n = rng.integers(0, CAP + 1, (N, 8))
    if how in ("comb", "full"): n[:] = CAP
    if how == "one": n[:] = 1
    if how == "none": n[int(rng.integers(N))] = 0; n[:, int(rng.integers(8))] = 0
    F = np.zeros((N, 8, T), np.int64)
    for r in range(N):
        for h in range(8):
            o = (rng.permutation(16)[:, None] + 16 * np.arange(T // 16)).reshape(-1) if how == "comb" else rng.permutation(T)
            F[r, h, o[:n[r, h]]] = 1
    if how == "run":
        p = rng.permutation(8); n[:, p[:2]] = CAP; n[:, p[2]] = CAP * rng.permutation(np.arange(N) % 2); n[:, p[3]] = 0
        s = rng.integers(0, T - n + 1); s[:, p[0]] = 0; s[:, p[1]] = T - CAP; s[:, p[2]] = 16 * rng.integers(0, max(1, (T - CAP) // 16), N) + 1
        F = ((np.arange(T) >= s[:, :, None]) & (np.arange(T) < (s + n)[:, :, None])).astype(np.int64)
    return {"keep": np.stack([np.concatenate([pack(F[r, h], 16) for h in range(8)], axis=0) for r in range(N)])}
def setup_inputs(rng):
    return dict({"x": rng.standard_normal((N, 128, T), dtype=np.float32)}, **lists(rng, "uniform"))
def setup_inputs_comb(rng):
    d = setup_inputs(rng); d.update(lists(rng, "comb"))
    for k in ("x",): d[k] = (d[k].astype(np.float32) * 1048576.0).astype(d[k].dtype)
    return d
def setup_inputs_full(rng):
    d = setup_inputs(rng); d.update(lists(rng, "full"))
    for k in ("x",): d[k] = (d[k].astype(np.float32) * (1 / 1024.0)).astype(d[k].dtype)
    return d
def setup_inputs_none(rng):
    d = setup_inputs(rng); d.update(lists(rng, "none"))
    return d
def setup_inputs_one(rng):
    d = setup_inputs(rng); d.update(lists(rng, "one"))
    return d
def setup_inputs_run(rng):
    d = setup_inputs(rng); d.update(lists(rng, "run"))
    return d
def check_inputs(x):
    bad = []
    if x["keep"].min() < 0 or x["keep"].max() >= 2: bad.append("keep out of range")
    if max(int(a[16 * h:16 * h + 16].sum()) for a in x["keep"] for h in range(8)) > CAP: bad.append("a head keeps more than CAP columns on a rank")
    return bad
def reference(x, keep):
    y = np.zeros((128, N * CAP), x.dtype)
    for h in range(8):
        H = slice(16 * h, 16 * h + 16); got = np.concatenate([x[r][H][:, entries(keep[r][H]) > 0] for r in range(N)], axis=1); y[H, :got.shape[1]] = got
    return {"y": np.broadcast_to(y, (N, 128, N * CAP))}

from concourse.bass import DstId, RemoteDMATransfer
from concourse.mybir import AluOpType as Op, ActivationFunctionType as Fn

TT, CAP, NR = 4096, 256, 3
NP = 128
A_N = 7
V_N = 16 - A_N

SCRATCH = {}
for _dt, _bufs in {
    "int32": {"kbuf": 256, "pint": 4},
    "uint16": {"off2": 16, "offt": 16, "offy": 48},
    "float32": {"xbuf": TT + 4, "land": NR * CAP + 4, "ybuf": NR * CAP, "cnt": 4 * NR, "pflt": 4, "iotn": 256,
                "md16": 128, "jw0": 48, "jw": 48, "jb": 16, "acc": A_N, "pwin": 260, "dcol": 4 * NR, "ecol": 4,
                "l0": 48, "l1": 48, "l2": 48, "l3": 48, "l4": 48, "l5": 48},
    "bfloat16": {"bones": 128, "ltri": 128, "utri": 128, "ehot": 144, "id16": 128, "rmask": V_N * NP, "flag": 256,
                 "ssum": 258, "cb": NP, "junk": A_N * NP, "cmp": V_N * NP, "scn": V_N * NP, "of2b": 16, "bits": 512},
}.items():
    for _n, _w in _bufs.items():
        SCRATCH[_n] = ("sbuf", [128, _w], _dt)
for _n in ("pca", "pcd", "pp", "pt"):
    SCRATCH[_n] = ("psum", [128, 512], "float32")
SEMAPHORES = ["v", "a", "p", "q", "ldk", "ldx", "st0", "st1", "carr", "darr", "loc"]


def rank_program(g, core, T, topo):
    rank = T.rank_of(core)
    if rank is None:
        return
    peers = [c for c in T.cores if c != core]
    V, A, P, S = g.vector, g.scalar, g.tensor, g.sync
    eng = {"v": V, "a": A, "p": P, "q": g, "s": S}
    issued = {"v": 0, "a": 0, "p": 0, "q": 0}
    seen = {}

    def need(queue, **sems):
        for s, n in sems.items():
            if seen.get((queue, s), 0) < n:
                eng[queue].wait_ge(T.sem[s], n)
                seen[(queue, s)] = n

    def did(queue, inst):
        inst.then_inc(T.sem[queue], 1)
        issued[queue] += 1
        return issued[queue]

    S.dma_start(T.kbuf[:], T.keep[:]).then_inc(T.sem.ldk, 16)
    S.dma_start(T.xbuf[:, 0:TT], T.x[:]).then_inc(T.sem.ldx, 16)

    g_p = did("q", g.iota(T.pint[:, 0:1], [[0, 1]], 0, 1))
    g_md = did("q", g.iota(T.md16[:], [[16, 8], [0, 16]], 0, 0, allow_small_or_imprecise_dtypes=True))
    g_jw = did("q", g.iota(T.jw0[:], [[16, 48]], 0, 0, allow_small_or_imprecise_dtypes=True))
    g_n = did("q", g.iota(T.iotn[:], [[1, 256]], 0, 0, allow_small_or_imprecise_dtypes=True))

    v = did("v", V.memset(T.rmask[:], 1.0))
    need("v", q=g_p)
    did("v", V.tensor_scalar(T.pint[:, 1:2], T.pint[:, 0:1], 15, None, Op.bitwise_and))
    v = did("v", V.tensor_scalar(T.pint[:, 2:3], T.pint[:, 0:1], 112, None, Op.bitwise_and))
    need("v", v=v)
    v = did("v", V.tensor_copy(T.pflt[:, 0:3], T.pint[:, 0:3]))
    did("v", V.memset(T.rmask[:, 0:V_N * NP:NP], 0.0))
    need("v", v=v, q=g_md)
    v_bo = did("v", V.tensor_scalar(T.bones[:], T.md16[:], T.pflt[:, 2:3], None, Op.is_equal))
    need("v", q=g_jw)
    did("v", V.tensor_scalar(T.jb[:], T.jw0[:, 0:16], T.pflt[:, 1:2], 0.5, Op.add, Op.add))
    need("q", v=v_bo)
    did("q", g.affine_select(T.ltri[:], T.bones[:], [[1, 128]], Op.is_ge, 0.0, 0, -1))
    g_ut = did("q", g.affine_select(T.utri[:], T.bones[:], [[-1, 128]], Op.is_gt, 0.0, 0, 1))
    did("v", V.memset(T.ssum[:, 0:1], 0.0))
    did("v", V.memset(T.pwin[:, 256:260], 1000.0))
    did("v", V.memset(T.land[:, NR * CAP:NR * CAP + 4], 0.0))
    did("v", V.memset(T.xbuf[:, TT:TT + 4], 0.0))
    need("v", q=g_n)
    did("v", V.tensor_scalar(T.ehot[:], T.iotn[:, 0:144], T.pflt[:, 2:3], 16.0, Op.subtract, Op.is_equal))
    did("v", V.tensor_scalar(T.id16[:], T.iotn[:, 0:128], T.pflt[:, 0:1], 16.0, Op.is_equal, Op.mult))
    v_const = did("v", V.tensor_scalar(T.jw[:], T.jw0[:], T.pflt[:, 1:2], None, Op.add))

    need("v", ldk=16)
    v = did("v", V.tensor_copy(T.flag[:], T.kbuf[:]))
    need("v", v=v)
    v = did("v", V.tensor_tensor_scan(T.ssum[:, 1:257], T.flag[:], T.flag[:], 0.0, Op.add, Op.max))
    need("p", v=v)
    p_ca = did("p", P.matmul(T.pca[:, 0:NP], T.bones[:], T.ssum[:, 2:257:2], True, True))
    p_cd = did("p", P.matmul(T.pcd[:, 0:NP], T.bones[:], T.ssum[:, 2:257:2], True, True))
    need("p", q=g_ut)
    did("p", P.matmul(T.pp[:, 0:256], T.ltri[:], T.ssum[:, 1:257], True, False))
    p_p = did("p", P.matmul(T.pp[:, 0:256], T.utri[:], T.ssum[:, 0:256], False, True))

    mine = T.cnt[:, 4 * rank:4 * rank + 1]
    need("a", v=v_const, p=p_ca)
    a_cnt = did("a", A.activation(mine, T.pca[:, NP - 1:NP], Fn.Copy))
    mask = topo.mask(core, peers[0]) & topo.mask(core, peers[1])
    n_eng = bin(mask).count("1")
    dst_ids = [DstId(rid=topo.addr(d)[0], pnc=topo.addr(d)[1]) for d in peers]
    need("q", a=a_cnt)
    g.remote_dma_fused([RemoteDMATransfer(dst_ids=dst_ids, dma_engine_mask=mask, remote_sem=T.sem.carr,
                                          srcs=[mine], dsts=[mine, mine])], local_sem=T.sem.loc)

    for k in range(A_N):
        a_s = did("a", A.activation(T.junk[:, k * NP:(k + 1) * NP], T.pca[:, 0:NP], Fn.Sign,
                                    bias=T.jb[:, k:k + 1], scale=-1.0, accum_out=T.acc[:, k:k + 1]))
    need("a", p=p_p)
    a_pw = did("a", A.activation(T.pwin[:, 0:256], T.pp[:, 0:256], Fn.Copy))

    need("v", p=p_cd)
    v = did("v", V.tensor_copy(T.cb[:], T.pcd[:, 0:NP]))
    need("v", v=v)
    for k in range(V_N):
        v = did("v", V.tensor_scalar(T.cmp[:, k * NP:(k + 1) * NP], T.cb[:], T.jb[:, A_N + k:A_N + k + 1], 2.0,
                                     Op.is_le, Op.mult))
    need("v", v=v)
    v_scn = did("v", V.tensor_tensor_scan(T.scn[:], T.rmask[:], T.cmp[:], 0.0, Op.mult, Op.add))
    need("v", a=a_s)
    did("v", V.tensor_scalar(T.off2[:, 0:A_N], T.acc[:], float(NP), None, Op.add))
    need("v", v=v_scn)
    v = did("v", V.tensor_copy(T.off2[:, A_N:16], T.scn[:, NP - 1:V_N * NP:NP]))
    need("a", a=a_s)
    did("a", A.activation(T.of2b[:, 0:A_N], T.acc[:], Fn.Identity, bias=float(NP)))
    need("a", v=v_scn)
    a_of = did("a", A.activation(T.of2b[:, A_N:16], T.scn[:, NP - 1:V_N * NP:NP], Fn.Copy))

    need("v", v=v, a=a_pw)
    v_b0 = did("v", V.tensor_tensor(T.bits[:, 0:256], T.pwin[:, 0:257].indirect(T.off2[:]), T.iotn[:], Op.is_le))
    v_b1 = did("v", V.tensor_tensor(T.bits[:, 256:512], T.pwin[:, 1:258].indirect(T.off2[:]), T.iotn[:], Op.is_le))
    need("p", a=a_of)
    did("p", P.matmul(T.pt[:, 0:16], T.id16[:], T.of2b[:], True, False))
    for half, vb in enumerate((v_b0, v_b1)):
        need("p", v=vb)
        for i in range(16):
            p_t = did("p", P.matmul(T.pt[:, 0:16], T.ehot[:, 16 - i:144 - i],
                                    T.bits[:, 256 * half + i:256 * half + 256:16], False, half == 1 and i == 15))
    need("v", p=p_t)
    v_off = did("v", V.tensor_copy(T.offt[:], T.pt[:, 0:16]))

    c0 = CAP * rank
    need("v", v=v_off, ldx=16)
    v_g = did("v", V.tensor_copy(T.land[:, c0:c0 + 128], T.xbuf[:, 0:TT + 4].indirect(T.offt[:, 0:8])))
    need("a", v=v_off, ldx=16)
    a_g = did("a", A.activation(T.land[:, c0 + 128:c0 + 256], T.xbuf[:, 0:TT + 4].indirect(T.offt[:, 8:16]), Fn.Copy))
    need("q", v=v_g, a=a_g)
    slot = T.land[:, c0:c0 + CAP]
    g.remote_dma_fused([RemoteDMATransfer(dst_ids=dst_ids, dma_engine_mask=mask, remote_sem=T.sem.darr,
                                          srcs=[slot], dsts=[slot, slot])], local_sem=T.sem.loc)

    need("v", carr=2 * n_eng, a=a_cnt)
    n0, n1, n2 = T.cnt[:, 0:1], T.cnt[:, 4:5], T.cnt[:, 8:9]
    did("v", V.tensor_scalar(T.dcol[:, 0:1], n0, -1.0, 256.0, Op.mult, Op.add))
    did("v", V.tensor_scalar(T.dcol[:, 4:5], n1, -1.0, 256.0, Op.mult, Op.add))
    v = did("v", V.tensor_tensor(T.ecol[:, 0:1], n0, n1, Op.add))
    need("v", v=v)
    v = did("v", V.tensor_tensor(T.ecol[:, 1:2], T.ecol[:, 0:1], n2, Op.add))
    did("v", V.tensor_scalar(T.l0[:], T.jw[:], n0, T.dcol[:, 0:1], Op.is_ge, Op.mult))
    did("v", V.tensor_scalar(T.l1[:], T.jw[:], T.ecol[:, 0:1], T.dcol[:, 4:5], Op.is_ge, Op.mult))
    need("v", v=v)
    v = did("v", V.tensor_scalar(T.l2[:], T.jw[:], T.ecol[:, 1:2], 1000.0, Op.is_ge, Op.mult))
    need("v", v=v)
    did("v", V.tensor_tensor(T.l3[:], T.l0[:], T.l1[:], Op.add))
    v = did("v", V.tensor_tensor(T.l4[:], T.l2[:], T.jw[:], Op.add))
    need("v", v=v)
    v = did("v", V.tensor_tensor(T.l5[:], T.l3[:], T.l4[:], Op.add))
    need("v", v=v)
    v = did("v", V.tensor_scalar(T.offy[:], T.l5[:], float(NR * CAP), None, Op.min))

    h = 24
    need("v", v=v, darr=2 * n_eng, a=a_g)
    v_y = did("v", V.tensor_copy(T.ybuf[:, 0:16 * h], T.land[:].indirect(T.offy[:, 0:h])))
    need("a", v=v, darr=2 * n_eng)
    need("a", a=a_g)
    a_y = did("a", A.activation(T.ybuf[:, 16 * h:768], T.land[:].indirect(T.offy[:, h:48]), Fn.Copy))
    need("s", v=v_y)
    S.dma_start(T.y[:, 0:16 * h], T.ybuf[:, 0:16 * h]).then_inc(T.sem.st0, 16)
    need("a", a=a_y)
    A.dma_start(T.y[:, 16 * h:768], T.ybuf[:, 16 * h:768]).then_inc(T.sem.st1, 16)
    S.wait_ge(T.sem.st0, 16)
    A.wait_ge(T.sem.st1, 16)
    need("q", loc=2 * n_eng, q=issued["q"], v=issued["v"], a=issued["a"], p=issued["p"])
